import numpy as np
import ml_dtypes


def mxq(x, axis, fmt="e4m3"):
    dtype, down = {"e4m3": (ml_dtypes.float8_e4m3fn, 7), "e5m2": (ml_dtypes.float8_e5m2, 14)}[fmt]
    v = np.moveaxis(np.asarray(x, np.float32).astype(ml_dtypes.bfloat16).astype(np.float64), axis, -1)
    blocks = v.reshape(v.shape[:-1] + (-1, 32))
    amax = np.abs(blocks).max(-1, keepdims=True)
    byte = np.maximum(np.where(amax > 0, np.frexp(amax)[1] - 1 + 127, 0) - down, 1)
    scale = np.exp2(byte - 127.0)
    codes = (blocks / scale).astype(np.float32).astype(dtype).astype(np.float64)
    return np.moveaxis((codes * scale).reshape(v.shape), -1, axis)


WIDE = False


def mx_kscale(k):
    if not WIDE:
        return np.ones(k)
    levels = np.array([10, -10, 5, -5, 0])
    if k % 512:
        return np.exp2(np.random.permutation(np.resize(levels, k // 32))).repeat(32)
    a = np.empty((k // 512, 16))
    for p in range(k // 512):
        a[p, :8] = np.random.permutation(np.resize(levels, 8))
        for g in range(8):
            far = levels[np.abs(levels - a[p, g]) >= 10]
            a[p, g + 8] = far[np.random.randint(len(far))]
    return np.exp2(a.ravel()).repeat(32)


def f64(x):
    return np.asarray(x).astype(np.float64)


def striped(idx):
    return np.tile(idx.reshape(-1, 16).T, (8, 1)).astype(np.uint16)


def unstriped(offs):
    return offs[:16].T.reshape(-1).astype(np.int64)


E2M1 = np.array([0.0, 0.5, 1.0, 1.5, 2.0, 3.0, 4.0, 6.0, -0.0, -0.5, -1.0, -1.5, -2.0, -3.0, -4.0, -6.0])


def pack_weight(w, fmt):
    k, n = w.shape
    w = f64(np.asarray(w, np.float32).astype(ml_dtypes.bfloat16)).reshape(k // 32, 32, n)
    amax = np.abs(w).max(1)
    if fmt == "e4m3":
        byte = np.frexp(amax)[1] - 1 + 127 - 7
    else:
        mant, ex = np.frexp(amax / 6.0)
        byte = np.where(mant > 0.5, ex, ex - 1) + 127
    byte = np.clip(np.where(amax > 0, byte, 1), 1, 254)
    scaled = (w * np.exp2(127.0 - byte)[:, None, :]).reshape(k, n).astype(np.float32)
    by_word = np.ascontiguousarray(scaled.reshape(k // 512, 128, 4, n).transpose(0, 1, 3, 2))
    if fmt == "e4m3":
        words = by_word.astype(ml_dtypes.float8_e4m3fn).view(np.uint8)
    else:
        c = by_word.astype(ml_dtypes.float4_e2m1fn).view(np.uint8) & 0xF
        words = (c[..., 0::2] | (c[..., 1::2] << 4)).reshape(k // 512, 128, 2 * n)
    return np.ascontiguousarray(words), np.ascontiguousarray(byte.astype(np.uint8).reshape(k // 512, 16, n))


def unpack_weight(words, scales, fmt):
    g, _, n = scales.shape
    words = np.ascontiguousarray(words).reshape(g, 128, n, -1)
    if fmt == "e4m3":
        vals = words.view(ml_dtypes.float8_e4m3fn).astype(np.float64)
    else:
        nib = np.empty((g, 128, n, 4), np.uint8)
        nib[..., 0::2] = words & 0xF
        nib[..., 1::2] = words >> 4
        vals = E2M1[nib]
    vals = vals * np.repeat(np.exp2(scales.astype(np.float64) - 127.0), 8, axis=1)[..., None]
    return vals.transpose(0, 1, 3, 2).reshape(g * 512, n)


def gelu(v):
    return 0.5 * v * (1.0 + np.tanh(np.sqrt(2.0 / np.pi) * (v + 0.044715 * v**3)))


K, T, H, S, T3, S2 = 1024, 2048, 1024, 512, 2048, 512

def setup_inputs():
    n = np.random.standard_normal
    s = mx_kscale(K)[:, None]
    u = mx_kscale(H)[:, None]
    tab_words, tab_scales = pack_weight(n((K, T)) * s, "e4m3")
    tab2_words, tab2_scales = pack_weight(n((H, T3)) / np.sqrt(H) / u, "e4m3")
    tab3_words, tab3_scales = pack_weight(n((H, T3)) / np.sqrt(H) / u, "e4m3")
    w2_words, w2_scales = pack_weight(n((K, H)) / np.sqrt(K) / s * u.T, "e2m1")
    return {
        "tab_words": tab_words, "tab_scales": tab_scales,
        "offs": striped(np.random.permutation(T)[:S]),
        "tab2_words": tab2_words, "tab2_scales": tab2_scales,
        "offs2": striped(np.random.permutation(T3)[:S2]),
        "tab3_words": tab3_words, "tab3_scales": tab3_scales,
        "offs3": striped(np.random.permutation(T3)[:S2]),
        "w1": (1.5 * n((K, H)) / np.sqrt(K) / s).astype(np.float32),
        "gain": (1.4 * np.exp(0.3 * n(H)) * u[:, 0]).astype(np.float32),
        "w2_words": w2_words, "w2_scales": w2_scales,
        "w3": (n((K, H)) / np.sqrt(K) / s * u.T).astype(np.float32),
        "weigh": np.exp(0.3 * n(S2)).astype(np.float32),
        "prior": (0.7 * n((S2, S))).astype(np.float32),
    }

def reference(tab_words, tab_scales, offs, tab2_words, tab2_scales, offs2, tab3_words, tab3_scales, offs3,
              w1, gain, w2_words, w2_scales, w3, weigh, prior):
    v = unpack_weight(tab_words, tab_scales, "e4m3")[:, unstriped(offs)]
    v2 = unpack_weight(tab2_words, tab2_scales, "e4m3")[:, unstriped(offs2)]
    v3 = unpack_weight(tab3_words, tab3_scales, "e4m3")[:, unstriped(offs3)]
    w2 = unpack_weight(w2_words, w2_scales, "e2m1")
    h = f64(gain)[:, None] * np.tanh(mxq(f64(w1), 0, "e4m3").T @ v)
    x = np.maximum(w2.T @ v, mxq(f64(w3), 0, "e4m3").T @ v)
    e = v2.T @ mxq(h, 0, "e4m3") + v3.T @ mxq(x, 0, "e4m3")
    score = 0.5 * e * (1.0 + np.tanh(np.sqrt(2.0 / np.pi) * (e + 0.044715 * e ** 3)))
    return f64(weigh)[:, None] * score + f64(prior)

@@ -1,0 +1,270 @@
+from contextlib import ExitStack
+
+import concourse.mybir as mybir
+
+F32 = mybir.dt.float32
+BF16 = mybir.dt.bfloat16
+I32 = mybir.dt.int32
+U32 = mybir.dt.uint32
+U16 = mybir.dt.uint16
+U8 = mybir.dt.uint8
+FP8X4 = mybir.dt.float8_e4m3fn_x4
+FP4X4 = mybir.dt.float4_e2m1fn_x4
+ACT = mybir.ActivationFunctionType
+ALU = mybir.AluOpType
+
+P = 128
+PACK = 4
+PASS = P * PACK
+PASSES = 2
+T = 2048
+S = 512
+QUADS = 4
+CHUNKS = S // P
+
+FLOPS = 2 * (3 * 1024 * 1024 * 512 + 2 * 1024 * 512 * 512)
+
+
+def tile_list_quartet_tutor_scores_kernel(
+    tc, tab_words, tab_scales, offs, tab2_words, tab2_scales, offs2, tab3_words, tab3_scales, offs3,
+    w1, gain, w2_words, w2_scales, w3, weigh, prior, out,
+):
+    nc = tc.nc
+    with ExitStack() as ctx:
+        keep = ctx.enter_context(tc.tile_pool(name="keep", bufs=1))
+        ring = ctx.enter_context(tc.tile_pool(name="ring", bufs=3))
+        psum = ctx.enter_context(tc.psum_pool(name="psum", bufs=1))
+
+        def held(name, shape, dtype):
+            return keep.tile(shape, dtype, name=name, align_bytes=64)
+
+        tab_sc = held("tab_sc", [P, PASSES, T], U8)
+        w2_sc_raw = held("w2_sc_raw", [P, PASSES, 1024], U8)
+        tab2_sc = held("tab2_sc", [P, T], U8)
+        tab3_sc = held("tab3_sc", [P, T], U8)
+        nc.vector.memset(tab_sc[:].bitcast(I32), 0)
+        nc.vector.memset(w2_sc_raw[:].bitcast(I32), 0)
+        nc.gpsimd.memset(tab2_sc[:].bitcast(I32), 0)
+        nc.gpsimd.memset(tab3_sc[:].bitcast(I32), 0)
+
+        raw = {}
+
+        def load_weight(name, w, a, b):
+            tile = held("raw_%s_%d_%d" % (name, a, b), [P, PACK, PASS], F32)
+            rows = w[a * PASS : (a + 1) * PASS, b * PASS : (b + 1) * PASS]
+            nc.sync.dma_start(out=tile[:], in_=rows.rearrange("(p j) c -> p j c", j=PACK))
+            raw[name, a, b] = tile
+
+        def load_words(name, words, a):
+            tile = held("%s_words_%d" % (name, a), [P, T], I32)
+            nc.sync.dma_start(out=tile[:], in_=words[a].rearrange("p t i -> p (t i)").bitcast(I32))
+            raw[name, a] = tile
+
+        def load_list(name, src):
+            tile = keep.tile([P, S // 16], U16, name=name)
+            nc.sync.dma_start(tile[:], src)
+            return tile
+
+        def load_scales_side_by_side(tile, scales):
+            src = scales.rearrange("a q c -> q a c").bitcast(I32)
+            for quad in range(QUADS):
+                nc.sync.dma_start(
+                    out=tile[:].bitcast(I32)[32 * quad : 32 * quad + 4], in_=src[4 * quad : 4 * quad + 4]
+                )
+
+        def load_scales_stacked(tile, scales, first):
+            src = scales.bitcast(I32)
+            for quad in range(QUADS):
+                row = 32 * quad + first
+                nc.sync.dma_start(
+                    out=tile[:].bitcast(I32)[row : row + 4 * PASSES], in_=src[:, 4 * quad : 4 * quad + 4, :]
+                )
+
+
+        list1 = load_list("list1", offs)
+        load_scales_side_by_side(tab_sc, tab_scales)
+        w2_raw = held("w2_raw", [P, PASSES, 2048], U8)
+        nc.sync.dma_start(out=w2_raw[:].bitcast(I32), in_=w2_words.rearrange("a p c -> p a c").bitcast(I32))
+        load_weight("w1", w1, 0, 0)
+        load_words("tab", tab_words, 0)
+        list2 = load_list("list2", offs2)
+        load_scales_side_by_side(w2_sc_raw, w2_scales)
+        load_words("tab", tab_words, 1)
+        load_weight("w1", w1, 1, 0)
+        load_scales_stacked(tab2_sc, tab2_scales, 4)
+        load_weight("w3", w3, 0, 0)
+        gain_sb = held("gain_sb", [P, PASSES, PACK], F32)
+        nc.sync.dma_start(out=gain_sb[:], in_=gain.rearrange("(b p t) -> p b t", b=PASSES, t=PACK))
+        load_weight("w3", w3, 1, 0)
+        list3 = load_list("list3", offs3)
+        load_scales_stacked(tab3_sc, tab3_scales, 8)
+        load_weight("w1", w1, 0, 1)
+        load_weight("w1", w1, 1, 1)
+        load_weight("w3", w3, 0, 1)
+        weigh_sb = held("weigh_sb", [P, CHUNKS], F32)
+        with nc.allow_non_contiguous_dma(reason="one factor for each output row"):
+            nc.sync.dma_start(out=weigh_sb[:], in_=weigh.rearrange("(i p) -> p i", p=P))
+        load_words("tab2", tab2_words, 0)
+        load_weight("w3", w3, 1, 1)
+        load_words("tab3", tab3_words, 0)
+        load_words("tab2", tab2_words, 1)
+        load_words("tab3", tab3_words, 1)
+
+        def gather_words(name, a, offsets):
+            picked = held("%s_picked_%d" % (name, a), [P, S], U32)
+            nc.vector.tensor_copy(picked[:], raw[name, a][:].bitcast(U32).indirect(offsets[:]))
+            return picked
+
+        def gather_bytes(name, window, offsets):
+            picked = held(name, [P, S], U8)
+            nc.vector.tensor_copy(picked[:], window.indirect(offsets[:]))
+            return picked
+
+        def quantise(name, grouped):
+            codes = held(name + "_codes", [P, S], U32)
+            scales = held(name + "_scales", [P, S], U8)
+            nc.vector.quantize_mx(out=codes[:].bitcast(FP8X4), scales=scales[:], in_=grouped[:])
+            return codes[:].bitcast(FP8X4), scales[:]
+
+        def round_weight(name, a, b):
+            grouped = ring.tile([P, PACK * PASS], BF16, name="w_grouped", align_bytes=64)
+            dst = grouped[:].rearrange("p (t m j) -> p m j t", t=PACK, j=PACK)
+            src = raw[name, a, b][:].rearrange("p j (m t) -> p m j t", t=PACK)
+            if b == 0:
+                nc.scalar.copy(out=dst[:, :, :, 0:2], in_=src[:, :, :, 0:2])
+                nc.vector.tensor_copy(out=dst[:, :, :, 2:4], in_=src[:, :, :, 2:4])
+            else:
+                nc.scalar.copy(out=dst, in_=src)
+            return quantise("%s_%d_%d" % (name, a, b), grouped)
+
+        weight_banks = [psum.tile([P, PACK, P], F32, name="weight_bank_%d" % c) for c in range(CHUNKS)]
+        side_banks = [psum.tile([P, PACK, P], F32, name="side_bank_%d" % c) for c in range(CHUNKS)]
+
+        def first_stage_pass(banks, a, weight):
+            codes, scales = weight
+            for c in range(CHUNKS):
+                cols = slice(c * P, (c + 1) * P)
+                for t in range(PACK):
+                    rows = slice(t * P, (t + 1) * P)
+                    nc.tensor.matmul_mx(
+                        out=banks[c][:, t, :],
+                        lhsT=codes[:, rows],
+                        lhsT_scale=scales[:, rows],
+                        rhs=v_words[a][:, cols].bitcast(FP8X4),
+                        rhs_scale=v_scales[a][:, cols],
+                        start=(a == 0 and t == 0),
+                        stop=(a == PASSES - 1 and t == PACK - 1),
+                    )
+
+        def woven(bank):
+            return bank[:].rearrange("p t n -> p n t")
+
+        def chunk(tile, c):
+            return tile[:, c * PASS : (c + 1) * PASS].rearrange("p (n t) -> p n t", t=PACK)
+
+        def w2_operand(a, b):
+            first = (a * PASSES + b) * PASS
+            return (
+                w2_dealt[:, 2 * first : 2 * (first + PASS)].bitcast(FP4X4),
+                w2_sc[:, first : first + PASS],
+            )
+
+        def w2_product(b):
+            for a in range(PASSES):
+                first_stage_pass(side_banks, a, w2_operand(a, b))
+
+        def keep_w2_product(b):
+            banks = side_banks
+            kept = held("w2_product_%d" % b, [P, CHUNKS * PASS], F32)
+            for c in range(CHUNKS):
+                nc.scalar.copy(out=chunk(kept, c), in_=woven(banks[c]))
+            return kept
+
+        def bound(banks):
+            tiles = []
+            for c in range(CHUNKS):
+                bounded = ring.tile([P, PASS], F32, name="bounded", bufs=8)
+                nc.scalar.activation(out=chunk(bounded, 0), in_=woven(banks[c]), func=ACT.Tanh)
+                tiles.append(bounded)
+            return tiles
+
+        def finish_h(tiles, b):
+            grouped = ring.tile([P, PACK * S], BF16, name="hx_grouped", align_bytes=64, bufs=3)
+            factor = gain_sb[:, b, :].unsqueeze(1).to_broadcast([P, P, PACK])
+            for c in range(CHUNKS):
+                nc.vector.tensor_tensor(out=chunk(grouped, c), in0=chunk(tiles[c], 0), in1=factor, op=ALU.mult)
+            return quantise("h_%d" % b, grouped)
+
+        def finish_x(banks, other, b):
+            grouped = ring.tile([P, PACK * S], BF16, name="hx_grouped", align_bytes=64, bufs=3)
+            for c in range(CHUNKS):
+                nc.vector.tensor_tensor(out=chunk(grouped, c), in0=woven(banks[c]), in1=chunk(other, c), op=ALU.max)
+            return quantise("x_%d" % b, grouped)
+
+        def second_stage_pass(words, scales, first_row, moving, start, stop):
+            codes, moving_scales = moving
+            for i in range(CHUNKS):
+                rows = slice(i * P, (i + 1) * P)
+                nc.tensor.matmul_mx(
+                    out=sums[i][:].rearrange("p t n -> p (t n)"),
+                    lhsT=words[:, rows].bitcast(FP8X4),
+                    lhsT_scale=scales[first_row:P, rows],
+                    rhs=codes,
+                    rhs_scale=moving_scales,
+                    start=start,
+                    stop=stop,
+                )
+
+        v_scales = [gather_bytes("v_scales_%d" % a, tab_sc[:, a, :], list1) for a in range(PASSES)]
+        w2_dealt = held("w2_dealt", [P, PASSES * 2048], U8)
+        nc.vector.tensor_copy(
+            out=w2_dealt[:].bitcast(U16).rearrange("p (g t m) -> p g t m", t=PACK, m=P),
+            in_=w2_raw[:].bitcast(U16).rearrange("p a (b m t) -> p (a b) t m", t=PACK, m=P),
+        )
+        v_words = [gather_words("tab", 0, list1)]
+        first_stage_pass(weight_banks, 0, round_weight("w1", 0, 0))
+        w2_sc = held("w2_sc", [P, PASSES * 1024], U8)
+        nc.vector.tensor_copy(
+            out=w2_sc[:].rearrange("p (g t m) -> p g t m", t=PACK, m=P),
+            in_=w2_sc_raw[:].rearrange("p a (b m t) -> p (a b) t m", t=PACK, m=P),
+        )
+        v_words.append(gather_words("tab", 1, list1))
+        first_stage_pass(weight_banks, 1, round_weight("w1", 1, 0))
+        w2_product(0)
+        bounded0 = bound(weight_banks)
+        first_stage_pass(weight_banks, 0, round_weight("w3", 0, 0))
+        first_stage_pass(weight_banks, 1, round_weight("w3", 1, 0))
+        a0 = keep_w2_product(0)
+        w2_product(1)
+        w1_01 = round_weight("w1", 0, 1)
+        h0 = finish_h(bounded0, 0)
+        x0 = finish_x(weight_banks, a0, 0)
+        first_stage_pass(weight_banks, 0, w1_01)
+        first_stage_pass(weight_banks, 1, round_weight("w1", 1, 1))
+        w3_01 = round_weight("w3", 0, 1)
+        bounded1 = bound(weight_banks)
+        first_stage_pass(weight_banks, 0, w3_01)
+        first_stage_pass(weight_banks, 1, round_weight("w3", 1, 1))
+        a1 = keep_w2_product(1)
+        h1 = finish_h(bounded1, 1)
+        x1 = finish_x(weight_banks, a1, 1)
+        v2_scales = gather_bytes("v2_scales", tab2_sc[:], list2)
+        v3_scales = gather_bytes("v3_scales", tab3_sc[:], list3)
+
+        sums = side_banks
+        second_stage_pass(gather_words("tab2", 0, list2), v2_scales, 4, h0, True, False)
+        second_stage_pass(gather_words("tab3", 0, list3), v3_scales, 8, x0, False, False)
+        second_stage_pass(gather_words("tab2", 1, list2), v2_scales, 8, h1, False, False)
+        second_stage_pass(gather_words("tab3", 1, list3), v3_scales, 12, x1, False, True)
+
+        prior_sb = held("raw_w1_0_0", [P, CHUNKS, S], F32)
+        for i in range(CHUNKS):
+            nc.sync.dma_start(out=prior_sb[:, i, :], in_=prior[i * P : (i + 1) * P, :])
+        for i in range(CHUNKS):
+            score = ring.tile([P, S], F32, name="bounded", bufs=8)
+            nc.scalar.activation(out=score[:], in_=sums[i][:].rearrange("p t n -> p (t n)"), func=ACT.Gelu_apprx_tanh)
+            nc.vector.scalar_tensor_tensor(
+                out=prior_sb[:, i, :], in0=score[:], scalar=weigh_sb[:, i : i + 1], in1=prior_sb[:, i, :],
+                op0=ALU.mult, op1=ALU.add,
+            )
+            nc.sync.dma_start(out=out[i * P : (i + 1) * P, :], in_=prior_sb[:, i, :])

@@ -21,6 +21,7 @@ T = 2048
 S = 512
 QUADS = 4
 CHUNKS = S // P
+ALL, MOST, HALF = 128, 96, 64
 
 FLOPS = 2 * (3 * 1024 * 1024 * 512 + 2 * 1024 * 512 * 512)
 
@@ -38,14 +39,19 @@ def tile_list_quartet_tutor_scores_kernel(
         def held(name, shape, dtype):
             return keep.tile(shape, dtype, name=name, align_bytes=64)
 
-        tab_sc = held("tab_sc", [P, PASSES, T], U8)
+        tab_sc = [held("tab_sc_%d" % a, [P, T], U8) for a in range(PASSES)]
         w2_sc_raw = held("w2_sc_raw", [P, PASSES, 1024], U8)
         tab2_sc = held("tab2_sc", [P, T], U8)
         tab3_sc = held("tab3_sc", [P, T], U8)
-        nc.vector.memset(tab_sc[:].bitcast(I32), 0)
+        nc.vector.memset(tab_sc[0][:].bitcast(I32), 0)
         nc.vector.memset(w2_sc_raw[:].bitcast(I32), 0)
+        nc.gpsimd.memset(tab_sc[1][:].bitcast(I32), 0)
         nc.gpsimd.memset(tab2_sc[:].bitcast(I32), 0)
-        nc.gpsimd.memset(tab3_sc[:].bitcast(I32), 0)
+        nc.vector.memset(tab3_sc[:].bitcast(I32), 0)
+
+        warm = held("warm", [P, 2], F32)
+        nc.vector.memset(warm[:, 0:1], 0.0)
+        nc.scalar.activation(out=warm[:, 1:2], in_=warm[:, 0:1], func=ACT.Gelu_apprx_tanh)
 
         raw = {}
 
@@ -66,11 +72,14 @@ def tile_list_quartet_tutor_scores_kernel(
             return tile
 
         def load_scales_side_by_side(tile, scales):
-            src = scales.rearrange("a q c -> q a c").bitcast(I32)
-            for quad in range(QUADS):
-                nc.sync.dma_start(
-                    out=tile[:].bitcast(I32)[32 * quad : 32 * quad + 4], in_=src[4 * quad : 4 * quad + 4]
-                )
+            src = scales.rearrange("a (quad r) c -> r quad a c", r=4).bitcast(I32)
+            for r in range(4):
+                nc.sync.dma_start(out=tile[:].bitcast(I32)[r:P:32], in_=src[r])
+
+        def load_scales_of_pass(tile, scales):
+            src = scales.rearrange("(quad r) c -> r quad c", r=4).bitcast(I32)
+            for r in range(4):
+                nc.sync.dma_start(out=tile[:].bitcast(I32)[r:P:32], in_=src[r])
 
         def load_scales_stacked(tile, scales, first):
             src = scales.bitcast(I32)
@@ -82,13 +91,15 @@ def tile_list_quartet_tutor_scores_kernel(
 
 
         list1 = load_list("list1", offs)
-        load_scales_side_by_side(tab_sc, tab_scales)
         w2_raw = held("w2_raw", [P, PASSES, 2048], U8)
         nc.sync.dma_start(out=w2_raw[:].bitcast(I32), in_=w2_words.rearrange("a p c -> p a c").bitcast(I32))
-        load_weight("w1", w1, 0, 0)
-        load_words("tab", tab_words, 0)
         list2 = load_list("list2", offs2)
+        list3 = load_list("list3", offs3)
+        load_scales_of_pass(tab_sc[0], tab_scales[0])
+        load_words("tab", tab_words, 0)
         load_scales_side_by_side(w2_sc_raw, w2_scales)
+        load_weight("w1", w1, 0, 0)
+        load_scales_of_pass(tab_sc[1], tab_scales[1])
         load_words("tab", tab_words, 1)
         load_weight("w1", w1, 1, 0)
         load_scales_stacked(tab2_sc, tab2_scales, 4)
@@ -96,19 +107,18 @@ def tile_list_quartet_tutor_scores_kernel(
         gain_sb = held("gain_sb", [P, PASSES, PACK], F32)
         nc.sync.dma_start(out=gain_sb[:], in_=gain.rearrange("(b p t) -> p b t", b=PASSES, t=PACK))
         load_weight("w3", w3, 1, 0)
-        list3 = load_list("list3", offs3)
         load_scales_stacked(tab3_sc, tab3_scales, 8)
         load_weight("w1", w1, 0, 1)
+        load_words("tab2", tab2_words, 0)
         load_weight("w1", w1, 1, 1)
         load_weight("w3", w3, 0, 1)
+        load_words("tab3", tab3_words, 0)
+        load_weight("w3", w3, 1, 1)
+        load_words("tab2", tab2_words, 1)
+        load_words("tab3", tab3_words, 1)
         weigh_sb = held("weigh_sb", [P, CHUNKS], F32)
         with nc.allow_non_contiguous_dma(reason="one factor for each output row"):
             nc.sync.dma_start(out=weigh_sb[:], in_=weigh.rearrange("(i p) -> p i", p=P))
-        load_words("tab2", tab2_words, 0)
-        load_weight("w3", w3, 1, 1)
-        load_words("tab3", tab3_words, 0)
-        load_words("tab2", tab2_words, 1)
-        load_words("tab3", tab3_words, 1)
 
         def gather_words(name, a, offsets):
             picked = held("%s_picked_%d" % (name, a), [P, S], U32)
@@ -120,22 +130,24 @@ def tile_list_quartet_tutor_scores_kernel(
             nc.vector.tensor_copy(picked[:], window.indirect(offsets[:]))
             return picked
 
-        def quantise(name, grouped):
-            codes = held(name + "_codes", [P, S], U32)
+        def quantise(name, grouped, codes_tag=None):
+            codes = held(codes_tag or name + "_codes", [P, S], U32)
             scales = held(name + "_scales", [P, S], U8)
             nc.vector.quantize_mx(out=codes[:].bitcast(FP8X4), scales=scales[:], in_=grouped[:])
             return codes[:].bitcast(FP8X4), scales[:]
 
-        def round_weight(name, a, b):
+        def round_weight(name, a, b, scalar_share):
             grouped = ring.tile([P, PACK * PASS], BF16, name="w_grouped", align_bytes=64)
             dst = grouped[:].rearrange("p (t m j) -> p m j t", t=PACK, j=PACK)
             src = raw[name, a, b][:].rearrange("p j (m t) -> p m j t", t=PACK)
-            if b == 0:
-                nc.scalar.copy(out=dst[:, :, :, 0:2], in_=src[:, :, :, 0:2])
-                nc.vector.tensor_copy(out=dst[:, :, :, 2:4], in_=src[:, :, :, 2:4])
-            else:
-                nc.scalar.copy(out=dst, in_=src)
-            return quantise("%s_%d_%d" % (name, a, b), grouped)
+            if scalar_share > 0:
+                nc.scalar.copy(out=dst[:, 0:scalar_share], in_=src[:, 0:scalar_share])
+            if scalar_share < P:
+                nc.vector.tensor_copy(out=dst[:, scalar_share:P], in_=src[:, scalar_share:P])
+            return grouped
+
+        def weight_operand(name, a, b, scalar_share):
+            return quantise("%s_%d_%d" % (name, a, b), round_weight(name, a, b, scalar_share))
 
         weight_banks = [psum.tile([P, PACK, P], F32, name="weight_bank_%d" % c) for c in range(CHUNKS)]
         side_banks = [psum.tile([P, PACK, P], F32, name="side_bank_%d" % c) for c in range(CHUNKS)]
@@ -169,12 +181,11 @@ def tile_list_quartet_tutor_scores_kernel(
                 w2_sc[:, first : first + PASS],
             )
 
-        def w2_product(b):
+        def w2_product(banks, b):
             for a in range(PASSES):
-                first_stage_pass(side_banks, a, w2_operand(a, b))
+                first_stage_pass(banks, a, w2_operand(a, b))
 
-        def keep_w2_product(b):
-            banks = side_banks
+        def keep_w2_product(banks, b):
             kept = held("w2_product_%d" % b, [P, CHUNKS * PASS], F32)
             for c in range(CHUNKS):
                 nc.scalar.copy(out=chunk(kept, c), in_=woven(banks[c]))
@@ -195,15 +206,15 @@ def tile_list_quartet_tutor_scores_kernel(
                 nc.vector.tensor_tensor(out=chunk(grouped, c), in0=chunk(tiles[c], 0), in1=factor, op=ALU.mult)
             return quantise("h_%d" % b, grouped)
 
-        def finish_x(banks, other, b):
+        def larger(banks, other):
             grouped = ring.tile([P, PACK * S], BF16, name="hx_grouped", align_bytes=64, bufs=3)
             for c in range(CHUNKS):
                 nc.vector.tensor_tensor(out=chunk(grouped, c), in0=woven(banks[c]), in1=chunk(other, c), op=ALU.max)
-            return quantise("x_%d" % b, grouped)
+            return grouped
 
-        def second_stage_pass(words, scales, first_row, moving, start, stop):
+        def second_stage_pass(words, scales, first_row, moving, start, stop, row_blocks=range(CHUNKS)):
             codes, moving_scales = moving
-            for i in range(CHUNKS):
+            for i in row_blocks:
                 rows = slice(i * P, (i + 1) * P)
                 nc.tensor.matmul_mx(
                     out=sums[i][:].rearrange("p t n -> p (t n)"),
@@ -215,47 +226,55 @@ def tile_list_quartet_tutor_scores_kernel(
                     stop=stop,
                 )
 
-        v_scales = [gather_bytes("v_scales_%d" % a, tab_sc[:, a, :], list1) for a in range(PASSES)]
         w2_dealt = held("w2_dealt", [P, PASSES * 2048], U8)
         nc.vector.tensor_copy(
             out=w2_dealt[:].bitcast(U16).rearrange("p (g t m) -> p g t m", t=PACK, m=P),
             in_=w2_raw[:].bitcast(U16).rearrange("p a (b m t) -> p (a b) t m", t=PACK, m=P),
         )
+        v_scales = [gather_bytes("v_scales_0", tab_sc[0][:], list1)]
         v_words = [gather_words("tab", 0, list1)]
-        first_stage_pass(weight_banks, 0, round_weight("w1", 0, 0))
         w2_sc = held("w2_sc", [P, PASSES * 1024], U8)
         nc.vector.tensor_copy(
             out=w2_sc[:].rearrange("p (g t m) -> p g t m", t=PACK, m=P),
             in_=w2_sc_raw[:].rearrange("p a (b m t) -> p (a b) t m", t=PACK, m=P),
         )
         v_words.append(gather_words("tab", 1, list1))
-        first_stage_pass(weight_banks, 1, round_weight("w1", 1, 0))
-        w2_product(0)
-        bounded0 = bound(weight_banks)
-        first_stage_pass(weight_banks, 0, round_weight("w3", 0, 0))
-        first_stage_pass(weight_banks, 1, round_weight("w3", 1, 0))
-        a0 = keep_w2_product(0)
-        w2_product(1)
-        w1_01 = round_weight("w1", 0, 1)
+        v_scales.append(gather_bytes("v_scales_1", tab_sc[1][:], list1))
+        w2_product(side_banks, 0)
+        w2_product(weight_banks, 1)
+        w1_00 = round_weight("w1", 0, 0, ALL)
+        a0 = keep_w2_product(side_banks, 0)
+        w1_10 = round_weight("w1", 1, 0, 0)
+        first_stage_pass(side_banks, 0, quantise("w1_0_0", w1_00, "tab_words_1"))
+        first_stage_pass(side_banks, 1, quantise("w1_1_0", w1_10))
+        a1 = keep_w2_product(weight_banks, 1)
+        first_stage_pass(weight_banks, 0, weight_operand("w3", 0, 0, 0))
+        first_stage_pass(weight_banks, 1, weight_operand("w3", 1, 0, ALL))
+        bounded0 = bound(side_banks)
+        first_stage_pass(side_banks, 0, weight_operand("w1", 0, 1, ALL))
+        first_stage_pass(side_banks, 1, weight_operand("w1", 1, 1, ALL))
+        x0 = larger(weight_banks, a0)
+        first_stage_pass(weight_banks, 0, weight_operand("w3", 0, 1, ALL))
+        bounded1 = bound(side_banks)
+        first_stage_pass(weight_banks, 1, weight_operand("w3", 1, 1, ALL))
         h0 = finish_h(bounded0, 0)
-        x0 = finish_x(weight_banks, a0, 0)
-        first_stage_pass(weight_banks, 0, w1_01)
-        first_stage_pass(weight_banks, 1, round_weight("w1", 1, 1))
-        w3_01 = round_weight("w3", 0, 1)
-        bounded1 = bound(weight_banks)
-        first_stage_pass(weight_banks, 0, w3_01)
-        first_stage_pass(weight_banks, 1, round_weight("w3", 1, 1))
-        a1 = keep_w2_product(1)
-        h1 = finish_h(bounded1, 1)
-        x1 = finish_x(weight_banks, a1, 1)
+        x0 = quantise("x_0", x0)
         v2_scales = gather_bytes("v2_scales", tab2_sc[:], list2)
         v3_scales = gather_bytes("v3_scales", tab3_sc[:], list3)
 
         sums = side_banks
         second_stage_pass(gather_words("tab2", 0, list2), v2_scales, 4, h0, True, False)
         second_stage_pass(gather_words("tab3", 0, list3), v3_scales, 8, x0, False, False)
-        second_stage_pass(gather_words("tab2", 1, list2), v2_scales, 8, h1, False, False)
-        second_stage_pass(gather_words("tab3", 1, list3), v3_scales, 12, x1, False, True)
+        picked = gather_words("tab2", 1, list2)
+        second_stage_pass(picked, v2_scales, 8, finish_h(bounded1, 1), False, False)
+        x1 = quantise("x_1", larger(weight_banks, a1))
+        last = held("tab3_picked_1", [P, S], U32)
+        for half in range(2):
+            nc.vector.tensor_copy(
+                last[:, half * S // 2 : (half + 1) * S // 2],
+                raw["tab3", 1][:].bitcast(U32).indirect(list3[:, half * S // 32 : (half + 1) * S // 32]),
+            )
+            second_stage_pass(last, v3_scales, 12, x1, False, True, range(2 * half, 2 * half + 2))
 
         prior_sb = held("raw_w1_0_0", [P, CHUNKS, S], F32)
         for i in range(CHUNKS):

@@ -39,14 +39,13 @@ def tile_list_quartet_tutor_scores_kernel(
         def held(name, shape, dtype):
             return keep.tile(shape, dtype, name=name, align_bytes=64)
 
-        tab_sc = [held("tab_sc_%d" % a, [P, T], U8) for a in range(PASSES)]
+        tab_sc = held("tab_sc", [P, PASSES, T], U8)
         w2_sc_raw = held("w2_sc_raw", [P, PASSES, 1024], U8)
         tab2_sc = held("tab2_sc", [P, T], U8)
         tab3_sc = held("tab3_sc", [P, T], U8)
-        nc.vector.memset(tab_sc[0][:].bitcast(I32), 0)
-        nc.vector.memset(w2_sc_raw[:].bitcast(I32), 0)
-        nc.gpsimd.memset(tab_sc[1][:].bitcast(I32), 0)
-        nc.gpsimd.memset(tab2_sc[:].bitcast(I32), 0)
+        nc.vector.memset(tab_sc[:].bitcast(I32), 0)
+        nc.gpsimd.memset(w2_sc_raw[:].bitcast(I32), 0)
+        nc.vector.memset(tab2_sc[:].bitcast(I32), 0)
         nc.vector.memset(tab3_sc[:].bitcast(I32), 0)
 
         warm = held("warm", [P, 2], F32)
@@ -71,43 +70,37 @@ def tile_list_quartet_tutor_scores_kernel(
             nc.sync.dma_start(tile[:], src)
             return tile
 
-        def load_scales_side_by_side(tile, scales):
+        def load_scales_side_by_side(queue, tile, scales):
             src = scales.rearrange("a (quad r) c -> r quad a c", r=4).bitcast(I32)
             for r in range(4):
-                nc.sync.dma_start(out=tile[:].bitcast(I32)[r:P:32], in_=src[r])
-
-        def load_scales_of_pass(tile, scales):
-            src = scales.rearrange("(quad r) c -> r quad c", r=4).bitcast(I32)
-            for r in range(4):
-                nc.sync.dma_start(out=tile[:].bitcast(I32)[r:P:32], in_=src[r])
+                queue.dma_start(out=tile[:].bitcast(I32)[r:P:32], in_=src[r])
 
         def load_scales_stacked(tile, scales, first):
             src = scales.bitcast(I32)
             for quad in range(QUADS):
                 row = 32 * quad + first
-                nc.sync.dma_start(
+                nc.gpsimd.dma_start(
                     out=tile[:].bitcast(I32)[row : row + 4 * PASSES], in_=src[:, 4 * quad : 4 * quad + 4, :]
                 )
 
 
         list1 = load_list("list1", offs)
+        list2 = load_list("list2", offs2)
+        load_scales_side_by_side(nc.sync, tab_sc, tab_scales)
+        load_scales_side_by_side(nc.gpsimd, w2_sc_raw, w2_scales)
+        load_scales_stacked(tab2_sc, tab2_scales, 4)
+        load_scales_stacked(tab3_sc, tab3_scales, 8)
         w2_raw = held("w2_raw", [P, PASSES, 2048], U8)
         nc.sync.dma_start(out=w2_raw[:].bitcast(I32), in_=w2_words.rearrange("a p c -> p a c").bitcast(I32))
-        list2 = load_list("list2", offs2)
-        list3 = load_list("list3", offs3)
-        load_scales_of_pass(tab_sc[0], tab_scales[0])
         load_words("tab", tab_words, 0)
-        load_scales_side_by_side(w2_sc_raw, w2_scales)
         load_weight("w1", w1, 0, 0)
-        load_scales_of_pass(tab_sc[1], tab_scales[1])
         load_words("tab", tab_words, 1)
-        load_weight("w1", w1, 1, 0)
-        load_scales_stacked(tab2_sc, tab2_scales, 4)
-        load_weight("w3", w3, 0, 0)
+        list3 = load_list("list3", offs3)
         gain_sb = held("gain_sb", [P, PASSES, PACK], F32)
         nc.sync.dma_start(out=gain_sb[:], in_=gain.rearrange("(b p t) -> p b t", b=PASSES, t=PACK))
+        load_weight("w1", w1, 1, 0)
+        load_weight("w3", w3, 0, 0)
         load_weight("w3", w3, 1, 0)
-        load_scales_stacked(tab3_sc, tab3_scales, 8)
         load_weight("w1", w1, 0, 1)
         load_words("tab2", tab2_words, 0)
         load_weight("w1", w1, 1, 1)
@@ -136,8 +129,9 @@ def tile_list_quartet_tutor_scores_kernel(
             nc.vector.quantize_mx(out=codes[:].bitcast(FP8X4), scales=scales[:], in_=grouped[:])
             return codes[:].bitcast(FP8X4), scales[:]
 
-        def round_weight(name, a, b, scalar_share):
-            grouped = ring.tile([P, PACK * PASS], BF16, name="w_grouped", align_bytes=64)
+        def round_weight(name, a, b, scalar_share, grouped=None):
+            if grouped is None:
+                grouped = ring.tile([P, PACK * PASS], BF16, name="w_grouped", align_bytes=64)
             dst = grouped[:].rearrange("p (t m j) -> p m j t", t=PACK, j=PACK)
             src = raw[name, a, b][:].rearrange("p j (m t) -> p m j t", t=PACK)
             if scalar_share > 0:
@@ -191,19 +185,17 @@ def tile_list_quartet_tutor_scores_kernel(
                 nc.scalar.copy(out=chunk(kept, c), in_=woven(banks[c]))
             return kept
 
-        def bound(banks):
-            tiles = []
+        def bound(banks, tag):
+            bounded = held(tag, [P, CHUNKS * PASS], F32)
             for c in range(CHUNKS):
-                bounded = ring.tile([P, PASS], F32, name="bounded", bufs=8)
-                nc.scalar.activation(out=chunk(bounded, 0), in_=woven(banks[c]), func=ACT.Tanh)
-                tiles.append(bounded)
-            return tiles
+                nc.scalar.activation(out=chunk(bounded, c), in_=woven(banks[c]), func=ACT.Tanh)
+            return bounded
 
-        def finish_h(tiles, b):
+        def finish_h(bounded, b):
             grouped = ring.tile([P, PACK * S], BF16, name="hx_grouped", align_bytes=64, bufs=3)
             factor = gain_sb[:, b, :].unsqueeze(1).to_broadcast([P, P, PACK])
             for c in range(CHUNKS):
-                nc.vector.tensor_tensor(out=chunk(grouped, c), in0=chunk(tiles[c], 0), in1=factor, op=ALU.mult)
+                nc.vector.tensor_tensor(out=chunk(grouped, c), in0=chunk(bounded, c), in1=factor, op=ALU.mult)
             return quantise("h_%d" % b, grouped)
 
         def larger(banks, other):
@@ -226,20 +218,18 @@ def tile_list_quartet_tutor_scores_kernel(
                     stop=stop,
                 )
 
+        v_scales = [gather_bytes("v_scales_%d" % a, tab_sc[:, a, :], list1) for a in range(PASSES)]
         w2_dealt = held("w2_dealt", [P, PASSES * 2048], U8)
         nc.vector.tensor_copy(
             out=w2_dealt[:].bitcast(U16).rearrange("p (g t m) -> p g t m", t=PACK, m=P),
             in_=w2_raw[:].bitcast(U16).rearrange("p a (b m t) -> p (a b) t m", t=PACK, m=P),
         )
-        v_scales = [gather_bytes("v_scales_0", tab_sc[0][:], list1)]
-        v_words = [gather_words("tab", 0, list1)]
-        w2_sc = held("w2_sc", [P, PASSES * 1024], U8)
+        w2_sc = held("tab_sc", [P, PASSES * 1024], U8)
         nc.vector.tensor_copy(
             out=w2_sc[:].rearrange("p (g t m) -> p g t m", t=PACK, m=P),
             in_=w2_sc_raw[:].rearrange("p a (b m t) -> p (a b) t m", t=PACK, m=P),
         )
-        v_words.append(gather_words("tab", 1, list1))
-        v_scales.append(gather_bytes("v_scales_1", tab_sc[1][:], list1))
+        v_words = [gather_words("tab", a, list1) for a in range(PASSES)]
         w2_product(side_banks, 0)
         w2_product(weight_banks, 1)
         w1_00 = round_weight("w1", 0, 0, ALL)
@@ -249,18 +239,19 @@ def tile_list_quartet_tutor_scores_kernel(
         first_stage_pass(side_banks, 1, quantise("w1_1_0", w1_10))
         a1 = keep_w2_product(weight_banks, 1)
         first_stage_pass(weight_banks, 0, weight_operand("w3", 0, 0, 0))
-        first_stage_pass(weight_banks, 1, weight_operand("w3", 1, 0, ALL))
-        bounded0 = bound(side_banks)
+        w3_10 = round_weight("w3", 1, 0, HALF, held("w3_1_0_grouped", [P, PACK * PASS], BF16))
+        first_stage_pass(weight_banks, 1, quantise("w3_1_0", w3_10))
+        bounded0 = bound(side_banks, "raw_w3_1_0")
         first_stage_pass(side_banks, 0, weight_operand("w1", 0, 1, ALL))
         first_stage_pass(side_banks, 1, weight_operand("w1", 1, 1, ALL))
         x0 = larger(weight_banks, a0)
         first_stage_pass(weight_banks, 0, weight_operand("w3", 0, 1, ALL))
-        bounded1 = bound(side_banks)
+        bounded1 = bound(side_banks, "bounded_1")
         first_stage_pass(weight_banks, 1, weight_operand("w3", 1, 1, ALL))
         h0 = finish_h(bounded0, 0)
         x0 = quantise("x_0", x0)
-        v2_scales = gather_bytes("v2_scales", tab2_sc[:], list2)
-        v3_scales = gather_bytes("v3_scales", tab3_sc[:], list3)
+        v2_scales = gather_bytes("raw_w1_1_0", tab2_sc[:], list2)
+        v3_scales = gather_bytes("w3_1_0_grouped", tab3_sc[:], list3)
 
         sums = side_banks
         second_stage_pass(gather_words("tab2", 0, list2), v2_scales, 4, h0, True, False)
@@ -280,7 +271,7 @@ def tile_list_quartet_tutor_scores_kernel(
         for i in range(CHUNKS):
             nc.sync.dma_start(out=prior_sb[:, i, :], in_=prior[i * P : (i + 1) * P, :])
         for i in range(CHUNKS):
-            score = ring.tile([P, S], F32, name="bounded", bufs=8)
+            score = ring.tile([P, S], F32, name="score", bufs=4)
             nc.scalar.activation(out=score[:], in_=sums[i][:].rearrange("p t n -> p (t n)"), func=ACT.Gelu_apprx_tanh)
             nc.vector.scalar_tensor_tensor(
                 out=prior_sb[:, i, :], in0=score[:], scalar=weigh_sb[:, i : i + 1], in1=prior_sb[:, i, :],

from contextlib import ExitStack

import concourse.mybir as mybir

F32 = mybir.dt.float32
BF16 = mybir.dt.bfloat16
I32 = mybir.dt.int32
U32 = mybir.dt.uint32
U16 = mybir.dt.uint16
U8 = mybir.dt.uint8
FP8X4 = mybir.dt.float8_e4m3fn_x4
FP4X4 = mybir.dt.float4_e2m1fn_x4
ACT = mybir.ActivationFunctionType
ALU = mybir.AluOpType

P = 128
PACK = 4
PASS = P * PACK
PASSES = 2
T = 2048
S = 512
QUADS = 4
CHUNKS = S // P
ALL, MOST, HALF = 128, 96, 64

FLOPS = 2 * (3 * 1024 * 1024 * 512 + 2 * 1024 * 512 * 512)


def tile_list_quartet_tutor_scores_kernel(
    tc, tab_words, tab_scales, offs, tab2_words, tab2_scales, offs2, tab3_words, tab3_scales, offs3,
    w1, gain, w2_words, w2_scales, w3, weigh, prior, out,
):
    nc = tc.nc
    with ExitStack() as ctx:
        keep = ctx.enter_context(tc.tile_pool(name="keep", bufs=1))
        ring = ctx.enter_context(tc.tile_pool(name="ring", bufs=3))
        psum = ctx.enter_context(tc.psum_pool(name="psum", bufs=1))

        def held(name, shape, dtype):
            return keep.tile(shape, dtype, name=name, align_bytes=64)

        tab_sc = held("tab_sc", [P, PASSES, T], U8)
        w2_sc_raw = held("w2_sc_raw", [P, PASSES, 1024], U8)
        tab2_sc = held("tab2_sc", [P, T], U8)
        tab3_sc = held("tab3_sc", [P, T], U8)
        nc.vector.memset(tab_sc[:].bitcast(I32), 0)
        nc.gpsimd.memset(w2_sc_raw[:].bitcast(I32), 0)
        nc.vector.memset(tab2_sc[:].bitcast(I32), 0)
        nc.vector.memset(tab3_sc[:].bitcast(I32), 0)

        warm = held("warm", [P, 2], F32)
        nc.vector.memset(warm[:, 0:1], 0.0)
        nc.scalar.activation(out=warm[:, 1:2], in_=warm[:, 0:1], func=ACT.Gelu_apprx_tanh)

        raw = {}

        def load_weight(name, w, a, b):
            tile = held("raw_%s_%d_%d" % (name, a, b), [P, PACK, PASS], F32)
            rows = w[a * PASS : (a + 1) * PASS, b * PASS : (b + 1) * PASS]
            nc.sync.dma_start(out=tile[:], in_=rows.rearrange("(p j) c -> p j c", j=PACK))
            raw[name, a, b] = tile

        def load_words(name, words, a):
            tile = held("%s_words_%d" % (name, a), [P, T], I32)
            nc.sync.dma_start(out=tile[:], in_=words[a].rearrange("p t i -> p (t i)").bitcast(I32))
            raw[name, a] = tile

        def load_list(name, src):
            tile = keep.tile([P, S // 16], U16, name=name)
            nc.sync.dma_start(tile[:], src)
            return tile

        def load_scales_side_by_side(queue, tile, scales):
            src = scales.rearrange("a (quad r) c -> r quad a c", r=4).bitcast(I32)
            for r in range(4):
                queue.dma_start(out=tile[:].bitcast(I32)[r:P:32], in_=src[r])

        def load_scales_stacked(tile, scales, first):
            src = scales.bitcast(I32)
            for quad in range(QUADS):
                row = 32 * quad + first
                nc.gpsimd.dma_start(
                    out=tile[:].bitcast(I32)[row : row + 4 * PASSES], in_=src[:, 4 * quad : 4 * quad + 4, :]
                )


        list1 = load_list("list1", offs)
        list2 = load_list("list2", offs2)
        load_scales_side_by_side(nc.sync, tab_sc, tab_scales)
        load_scales_side_by_side(nc.gpsimd, w2_sc_raw, w2_scales)
        load_scales_stacked(tab2_sc, tab2_scales, 4)
        load_scales_stacked(tab3_sc, tab3_scales, 8)
        w2_raw = held("w2_raw", [P, PASSES, 2048], U8)
        nc.sync.dma_start(out=w2_raw[:].bitcast(I32), in_=w2_words.rearrange("a p c -> p a c").bitcast(I32))
        load_words("tab", tab_words, 0)
        load_weight("w1", w1, 0, 0)
        load_words("tab", tab_words, 1)
        list3 = load_list("list3", offs3)
        gain_sb = held("gain_sb", [P, PASSES, PACK], F32)
        nc.sync.dma_start(out=gain_sb[:], in_=gain.rearrange("(b p t) -> p b t", b=PASSES, t=PACK))
        load_weight("w1", w1, 1, 0)
        load_weight("w3", w3, 0, 0)
        load_weight("w3", w3, 1, 0)
        load_weight("w1", w1, 0, 1)
        load_words("tab2", tab2_words, 0)
        load_weight("w1", w1, 1, 1)
        load_weight("w3", w3, 0, 1)
        load_words("tab3", tab3_words, 0)
        load_weight("w3", w3, 1, 1)
        load_words("tab2", tab2_words, 1)
        load_words("tab3", tab3_words, 1)
        weigh_sb = held("weigh_sb", [P, CHUNKS], F32)
        with nc.allow_non_contiguous_dma(reason="one factor for each output row"):
            nc.sync.dma_start(out=weigh_sb[:], in_=weigh.rearrange("(i p) -> p i", p=P))

        def gather_words(name, a, offsets):
            picked = held("%s_picked_%d" % (name, a), [P, S], U32)
            nc.vector.tensor_copy(picked[:], raw[name, a][:].bitcast(U32).indirect(offsets[:]))
            return picked

        def gather_bytes(name, window, offsets):
            picked = held(name, [P, S], U8)
            nc.vector.tensor_copy(picked[:], window.indirect(offsets[:]))
            return picked

        def quantise(name, grouped, codes_tag=None):
            codes = held(codes_tag or name + "_codes", [P, S], U32)
            scales = held(name + "_scales", [P, S], U8)
            nc.vector.quantize_mx(out=codes[:].bitcast(FP8X4), scales=scales[:], in_=grouped[:])
            return codes[:].bitcast(FP8X4), scales[:]

        def round_weight(name, a, b, scalar_share, grouped=None):
            if grouped is None:
                grouped = ring.tile([P, PACK * PASS], BF16, name="w_grouped", align_bytes=64)
            dst = grouped[:].rearrange("p (t m j) -> p m j t", t=PACK, j=PACK)
            src = raw[name, a, b][:].rearrange("p j (m t) -> p m j t", t=PACK)
            if scalar_share > 0:
                nc.scalar.copy(out=dst[:, 0:scalar_share], in_=src[:, 0:scalar_share])
            if scalar_share < P:
                nc.vector.tensor_copy(out=dst[:, scalar_share:P], in_=src[:, scalar_share:P])
            return grouped

        def weight_operand(name, a, b, scalar_share):
            return quantise("%s_%d_%d" % (name, a, b), round_weight(name, a, b, scalar_share))

        weight_banks = [psum.tile([P, PACK, P], F32, name="weight_bank_%d" % c) for c in range(CHUNKS)]
        side_banks = [psum.tile([P, PACK, P], F32, name="side_bank_%d" % c) for c in range(CHUNKS)]

        def first_stage_pass(banks, a, weight):
            codes, scales = weight
            for c in range(CHUNKS):
                cols = slice(c * P, (c + 1) * P)
                for t in range(PACK):
                    rows = slice(t * P, (t + 1) * P)
                    nc.tensor.matmul_mx(
                        out=banks[c][:, t, :],
                        lhsT=codes[:, rows],
                        lhsT_scale=scales[:, rows],
                        rhs=v_words[a][:, cols].bitcast(FP8X4),
                        rhs_scale=v_scales[a][:, cols],
                        start=(a == 0 and t == 0),
                        stop=(a == PASSES - 1 and t == PACK - 1),
                    )

        def woven(bank):
            return bank[:].rearrange("p t n -> p n t")

        def chunk(tile, c):
            return tile[:, c * PASS : (c + 1) * PASS].rearrange("p (n t) -> p n t", t=PACK)

        def w2_operand(a, b):
            first = (a * PASSES + b) * PASS
            return (
                w2_dealt[:, 2 * first : 2 * (first + PASS)].bitcast(FP4X4),
                w2_sc[:, first : first + PASS],
            )

        def w2_product(banks, b):
            for a in range(PASSES):
                first_stage_pass(banks, a, w2_operand(a, b))

        def keep_w2_product(banks, b):
            kept = held("w2_product_%d" % b, [P, CHUNKS * PASS], F32)
            for c in range(CHUNKS):
                nc.scalar.copy(out=chunk(kept, c), in_=woven(banks[c]))
            return kept

        def bound(banks, tag):
            bounded = held(tag, [P, CHUNKS * PASS], F32)
            for c in range(CHUNKS):
                nc.scalar.activation(out=chunk(bounded, c), in_=woven(banks[c]), func=ACT.Tanh)
            return bounded

        def finish_h(bounded, b):
            grouped = ring.tile([P, PACK * S], BF16, name="hx_grouped", align_bytes=64, bufs=3)
            factor = gain_sb[:, b, :].unsqueeze(1).to_broadcast([P, P, PACK])
            for c in range(CHUNKS):
                nc.vector.tensor_tensor(out=chunk(grouped, c), in0=chunk(bounded, c), in1=factor, op=ALU.mult)
            return quantise("h_%d" % b, grouped)

        def larger(banks, other):
            grouped = ring.tile([P, PACK * S], BF16, name="hx_grouped", align_bytes=64, bufs=3)
            for c in range(CHUNKS):
                nc.vector.tensor_tensor(out=chunk(grouped, c), in0=woven(banks[c]), in1=chunk(other, c), op=ALU.max)
            return grouped

        def second_stage_pass(words, scales, first_row, moving, start, stop, row_blocks=range(CHUNKS)):
            codes, moving_scales = moving
            for i in row_blocks:
                rows = slice(i * P, (i + 1) * P)
                nc.tensor.matmul_mx(
                    out=sums[i][:].rearrange("p t n -> p (t n)"),
                    lhsT=words[:, rows].bitcast(FP8X4),
                    lhsT_scale=scales[first_row:P, rows],
                    rhs=codes,
                    rhs_scale=moving_scales,
                    start=start,
                    stop=stop,
                )

        v_scales = [gather_bytes("v_scales_%d" % a, tab_sc[:, a, :], list1) for a in range(PASSES)]
        w2_dealt = held("w2_dealt", [P, PASSES * 2048], U8)
        nc.vector.tensor_copy(
            out=w2_dealt[:].bitcast(U16).rearrange("p (g t m) -> p g t m", t=PACK, m=P),
            in_=w2_raw[:].bitcast(U16).rearrange("p a (b m t) -> p (a b) t m", t=PACK, m=P),
        )
        w2_sc = held("tab_sc", [P, PASSES * 1024], U8)
        nc.vector.tensor_copy(
            out=w2_sc[:].rearrange("p (g t m) -> p g t m", t=PACK, m=P),
            in_=w2_sc_raw[:].rearrange("p a (b m t) -> p (a b) t m", t=PACK, m=P),
        )
        v_words = [gather_words("tab", a, list1) for a in range(PASSES)]
        w2_product(side_banks, 0)
        w2_product(weight_banks, 1)
        w1_00 = round_weight("w1", 0, 0, ALL)
        a0 = keep_w2_product(side_banks, 0)
        w1_10 = round_weight("w1", 1, 0, 0)
        first_stage_pass(side_banks, 0, quantise("w1_0_0", w1_00, "tab_words_1"))
        first_stage_pass(side_banks, 1, quantise("w1_1_0", w1_10))
        a1 = keep_w2_product(weight_banks, 1)
        first_stage_pass(weight_banks, 0, weight_operand("w3", 0, 0, 0))
        w3_10 = round_weight("w3", 1, 0, HALF, held("w3_1_0_grouped", [P, PACK * PASS], BF16))
        first_stage_pass(weight_banks, 1, quantise("w3_1_0", w3_10))
        bounded0 = bound(side_banks, "raw_w3_1_0")
        first_stage_pass(side_banks, 0, weight_operand("w1", 0, 1, ALL))
        first_stage_pass(side_banks, 1, weight_operand("w1", 1, 1, ALL))
        x0 = larger(weight_banks, a0)
        first_stage_pass(weight_banks, 0, weight_operand("w3", 0, 1, ALL))
        bounded1 = bound(side_banks, "bounded_1")
        first_stage_pass(weight_banks, 1, weight_operand("w3", 1, 1, ALL))
        h0 = finish_h(bounded0, 0)
        x0 = quantise("x_0", x0)
        v2_scales = gather_bytes("raw_w1_1_0", tab2_sc[:], list2)
        v3_scales = gather_bytes("w3_1_0_grouped", tab3_sc[:], list3)

        sums = side_banks
        second_stage_pass(gather_words("tab2", 0, list2), v2_scales, 4, h0, True, False)
        second_stage_pass(gather_words("tab3", 0, list3), v3_scales, 8, x0, False, False)
        picked = gather_words("tab2", 1, list2)
        second_stage_pass(picked, v2_scales, 8, finish_h(bounded1, 1), False, False)
        x1 = quantise("x_1", larger(weight_banks, a1))
        last = held("tab3_picked_1", [P, S], U32)
        for half in range(2):
            nc.vector.tensor_copy(
                last[:, half * S // 2 : (half + 1) * S // 2],
                raw["tab3", 1][:].bitcast(U32).indirect(list3[:, half * S // 32 : (half + 1) * S // 32]),
            )
            second_stage_pass(last, v3_scales, 12, x1, False, True, range(2 * half, 2 * half + 2))

        prior_sb = held("raw_w1_0_0", [P, CHUNKS, S], F32)
        for i in range(CHUNKS):
            nc.sync.dma_start(out=prior_sb[:, i, :], in_=prior[i * P : (i + 1) * P, :])
        for i in range(CHUNKS):
            score = ring.tile([P, S], F32, name="score", bufs=4)
            nc.scalar.activation(out=score[:], in_=sums[i][:].rearrange("p t n -> p (t n)"), func=ACT.Gelu_apprx_tanh)
            nc.vector.scalar_tensor_tensor(
                out=prior_sb[:, i, :], in0=score[:], scalar=weigh_sb[:, i : i + 1], in1=prior_sb[:, i, :],
                op0=ALU.mult, op1=ALU.add,
            )
            nc.sync.dma_start(out=out[i * P : (i + 1) * P, :], in_=prior_sb[:, i, :])
